import numpy as np
import ml_dtypes


def mxq(x, axis, fmt="e4m3"):
    dtype, down = {"e4m3": (ml_dtypes.float8_e4m3fn, 7), "e5m2": (ml_dtypes.float8_e5m2, 14)}[fmt]
    v = np.moveaxis(np.asarray(x, np.float32).astype(ml_dtypes.bfloat16).astype(np.float64), axis, -1)
    blocks = v.reshape(v.shape[:-1] + (-1, 32))
    amax = np.abs(blocks).max(-1, keepdims=True)
    byte = np.maximum(np.where(amax > 0, np.frexp(amax)[1] - 1 + 127, 0) - down, 1)
    scale = np.exp2(byte - 127.0)
    codes = (blocks / scale).astype(np.float32).astype(dtype).astype(np.float64)
    return np.moveaxis((codes * scale).reshape(v.shape), -1, axis)


WIDE = False


def mx_kscale(k):
    if not WIDE:
        return np.ones(k)
    levels = np.array([10, -10, 5, -5, 0])
    if k % 512:
        return np.exp2(np.random.permutation(np.resize(levels, k // 32))).repeat(32)
    a = np.empty((k // 512, 16))
    for p in range(k // 512):
        a[p, :8] = np.random.permutation(np.resize(levels, 8))
        for g in range(8):
            far = levels[np.abs(levels - a[p, g]) >= 10]
            a[p, g + 8] = far[np.random.randint(len(far))]
    return np.exp2(a.ravel()).repeat(32)


def f64(x):
    return np.asarray(x).astype(np.float64)


def striped8(idx):
    return np.concatenate([v.reshape(-1, 16).T for v in idx]).astype(np.uint16)


def unstriped8(offs):
    return np.stack([offs[16 * g:16 * g + 16].T.reshape(-1) for g in range(8)]).astype(np.int64)


E2M1 = np.array([0.0, 0.5, 1.0, 1.5, 2.0, 3.0, 4.0, 6.0, -0.0, -0.5, -1.0, -1.5, -2.0, -3.0, -4.0, -6.0])


def pack_weight(w, fmt):
    k, n = w.shape
    w = f64(np.asarray(w, np.float32).astype(ml_dtypes.bfloat16)).reshape(k // 32, 32, n)
    amax = np.abs(w).max(1)
    if fmt == "e4m3":
        byte = np.frexp(amax)[1] - 1 + 127 - 7
    else:
        mant, ex = np.frexp(amax / 6.0)
        byte = np.where(mant > 0.5, ex, ex - 1) + 127
    byte = np.clip(np.where(amax > 0, byte, 1), 1, 254)
    scaled = (w * np.exp2(127.0 - byte)[:, None, :]).reshape(k, n).astype(np.float32)
    by_word = np.ascontiguousarray(scaled.reshape(k // 512, 128, 4, n).transpose(0, 1, 3, 2))
    if fmt == "e4m3":
        words = by_word.astype(ml_dtypes.float8_e4m3fn).view(np.uint8)
    else:
        c = by_word.astype(ml_dtypes.float4_e2m1fn).view(np.uint8) & 0xF
        words = (c[..., 0::2] | (c[..., 1::2] << 4)).reshape(k // 512, 128, 2 * n)
    return np.ascontiguousarray(words), np.ascontiguousarray(byte.astype(np.uint8).reshape(k // 512, 16, n))


def unpack_weight(words, scales, fmt):
    g, _, n = scales.shape
    words = np.ascontiguousarray(words).reshape(g, 128, n, -1)
    if fmt == "e4m3":
        vals = words.view(ml_dtypes.float8_e4m3fn).astype(np.float64)
    else:
        nib = np.empty((g, 128, n, 4), np.uint8)
        nib[..., 0::2] = words & 0xF
        nib[..., 1::2] = words >> 4
        vals = E2M1[nib]
    vals = vals * np.repeat(np.exp2(scales.astype(np.float64) - 127.0), 8, axis=1)[..., None]
    return vals.transpose(0, 1, 3, 2).reshape(g * 512, n)


K, M, T, S = 512, 256, 2048, 1024


def setup_inputs():
    n = np.random.standard_normal
    s = mx_kscale(K)[:, None]
    w = n((K, M)) / np.sqrt(K) / s
    w4 = pack_weight(w, "e2m1")
    rest = w - unpack_weight(*w4, "e2m1")
    p_r8 = pack_weight(rest, "e4m3")
    return {
        "xT": (n((K, T)) * s).astype(np.float32),
        "w4_words": w4[0],
        "w4_scales": w4[1],
        "r8_words": p_r8[0],
        "r8_scales": p_r8[1],
        "wgt": np.repeat(np.random.uniform(0.5, 2.0, (8, S)), 16, axis=0).astype(np.float32),
        "offs": striped8(np.stack([np.random.permutation(T)[:S] for _ in range(8)])),
    }


def reference(xT, w4_words, w4_scales, r8_words, r8_scales, wgt, offs):
    idx = unstriped8(offs)
    group = np.arange(K) % 512 // 64
    xg = f64(wgt)[np.arange(K) // 4 % 128] * f64(xT)[np.arange(K)[:, None], idx[group]]
    xT_ = mxq(xg, 0, "e4m3")
    w4_ = unpack_weight(w4_words, w4_scales, "e2m1")
    r8_ = unpack_weight(r8_words, r8_scales, "e4m3")
    y = w4_.T @ xT_ + r8_.T @ xT_
    return y

@@ -1,0 +1,120 @@
+from contextlib import ExitStack
+
+import concourse.mybir as mybir
+
+K, M, T, S = 512, 256, 2048, 1024
+FLOPS = 2 * 2 * K * M * S
+
+F32 = mybir.dt.float32
+BF16 = mybir.dt.bfloat16
+I32 = mybir.dt.int32
+U32 = mybir.dt.uint32
+U16 = mybir.dt.uint16
+U8 = mybir.dt.uint8
+FP8X4 = mybir.dt.float8_e4m3fn_x4
+FP4X4 = mybir.dt.float4_e2m1fn_x4
+MULT = mybir.AluOpType.mult
+
+P = 128
+PACK = 4
+
+
+def tile_list_heads_none_kernel(
+    tc, xT, w4_words, w4_scales, r8_words, r8_scales, wgt, offs, out
+):
+    nc = tc.nc
+    planes = xT.rearrange("(p i) t -> i p t", i=PACK)
+
+    with ExitStack() as ctx:
+        lists = ctx.enter_context(tc.tile_pool(name="lists", bufs=1))
+        keep = ctx.enter_context(tc.tile_pool(name="keep", bufs=1))
+        psum = ctx.enter_context(tc.psum_pool(name="psum", bufs=1))
+
+        offsets = lists.tile([P, S // 16], U16, name="offsets")
+        weight = keep.tile([P, S], F32, name="weight", align_bytes=64)
+        xs = [keep.tile([P, T], F32, name=f"x{i}", align_bytes=64) for i in range(PACK)]
+        w4 = keep.tile([P, 2 * M], U8, name="w4", align_bytes=64)
+        r8 = keep.tile([P, M], U32, name="r8", align_bytes=64)
+        w4s = keep.tile([P, M], U8, name="w4s", align_bytes=64)
+        r8s = keep.tile([P, M], U8, name="r8s", align_bytes=64)
+        g = [keep.tile([P, 2, S], F32, name=f"g{h}", align_bytes=64) for h in range(2)]
+        xb = keep.tile([P, S, PACK], BF16, name="xb", align_bytes=64)
+        codes = keep.tile([P, S], U32, name="codes", align_bytes=64)
+        scales = keep.tile([P, S], U8, name="scales", align_bytes=64)
+
+        nc.vector.memset(r8s[:].bitcast(I32), 0)
+        nc.vector.memset(w4s[:].bitcast(I32), 0)
+
+        nc.sync.dma_start(offsets[:], offs)
+        nc.sync.dma_start(weight[:, 0:256], wgt[:, 0:256])
+        nc.sync.dma_start(xs[0][:], planes[0])
+        nc.sync.dma_start(weight[:, 256:1024], wgt[:, 256:1024])
+        for q in range(4):
+            nc.gpsimd.dma_start(
+                r8s[32 * q : 32 * q + 4, :].bitcast(I32), r8_scales[0, 4 * q : 4 * q + 4, :].bitcast(I32)
+            )
+        for i in range(1, PACK):
+            nc.sync.dma_start(xs[i][:], planes[i])
+        for q in range(4):
+            nc.gpsimd.dma_start(
+                w4s[32 * q : 32 * q + 4, :].bitcast(I32), w4_scales[0, 4 * q : 4 * q + 4, :].bitcast(I32)
+            )
+        nc.sync.dma_start(r8[:].bitcast(I32), r8_words[0].rearrange("p n t -> p (n t)").bitcast(I32))
+        nc.sync.dma_start(w4[:].bitcast(I32), w4_words[0].bitcast(I32))
+
+        def gather(i, a, b):
+            nc.vector.tensor_tensor(
+                g[i // 2][:, i % 2, a:b], xs[i][:].indirect(offsets[:, a // 16 : b // 16]), weight[:, a:b], MULT
+            )
+
+        def interleave(copy, h, a, b):
+            copy(xb[:, a:b, 2 * h : 2 * h + 2], g[h][:, :, a:b].rearrange("p t n -> p n t"))
+
+        for i in range(3):
+            if i == 0:
+                gather(i, 0, 256)
+                gather(i, 256, 512)
+            else:
+                gather(i, 0, 512)
+            gather(i, 512, 1024)
+            if i == 1:
+                interleave(nc.scalar.copy, 0, 0, 512)
+                interleave(nc.scalar.copy, 0, 512, 1024)
+
+        chunks = ((0, 256, nc.scalar.copy), (256, 256, nc.scalar.copy), (512, 256, nc.scalar.copy), (768, 256, nc.vector.tensor_copy))
+        for a, w, copy in chunks:
+            gather(3, a, a + w)
+            interleave(copy, 1, a, a + w)
+            nc.vector.quantize_mx(
+                out=codes[:, a : a + w].bitcast(FP8X4),
+                scales=scales[:, a : a + w],
+                in_=xb[:, a : a + w, :].rearrange("p n t -> p (n t)"),
+            )
+            for m in range(2):
+                acc = psum.tile([P, w], F32, name=f"acc{a}_{m}")
+                for b in range(0, w, 128):
+                    cols = slice(a + b, a + b + 128)
+                    nc.tensor.matmul_mx(
+                        out=acc[:, b : b + 128],
+                        lhsT=w4[:, 256 * m : 256 * m + 256].bitcast(FP4X4),
+                        lhsT_scale=w4s[:, 128 * m : 128 * m + 128],
+                        rhs=codes[:, cols].bitcast(FP8X4),
+                        rhs_scale=scales[:, cols],
+                        start=True,
+                        stop=False,
+                    )
+                    nc.tensor.matmul_mx(
+                        out=acc[:, b : b + 128],
+                        lhsT=r8[:, 128 * m : 128 * m + 128].bitcast(FP8X4),
+                        lhsT_scale=r8s[:, 128 * m : 128 * m + 128],
+                        rhs=codes[:, cols].bitcast(FP8X4),
+                        rhs_scale=scales[:, cols],
+                        start=False,
+                        stop=True,
+                    )
+                res = keep.tile([P, w], F32, name=f"res{a}_{m}", align_bytes=64)
+                if m == 0:
+                    nc.scalar.copy(res[:], acc[:])
+                else:
+                    nc.vector.tensor_copy(res[:], acc[:])
+                nc.sync.dma_start(out[128 * m : 128 * m + 128, a : a + w], res[:])

@@ -1,6 +1,7 @@
 from contextlib import ExitStack
 
 import concourse.mybir as mybir
+from concourse.masks import make_identity
 
 K, M, T, S = 512, 256, 2048, 1024
 FLOPS = 2 * 2 * K * M * S
@@ -42,25 +43,35 @@ def tile_list_heads_none_kernel(
         codes = keep.tile([P, S], U32, name="codes", align_bytes=64)
         scales = keep.tile([P, S], U8, name="scales", align_bytes=64)
 
+        ident = keep.tile([P, P], F32, name="ident", align_bytes=64)
+        make_identity(nc, ident[:])
+        warm = psum.tile([P, 256], F32, name="acc768_1")
+
+        def warm_up(src):
+            nc.tensor.transpose(warm[:, 0:128], src, ident[:])
+
         nc.vector.memset(r8s[:].bitcast(I32), 0)
         nc.vector.memset(w4s[:].bitcast(I32), 0)
+
+        def load_scales(engine, tile, src, q):
+            engine.dma_start(tile[32 * q : 32 * q + 4, :].bitcast(I32), src[0, 4 * q : 4 * q + 4, :].bitcast(I32))
 
         nc.sync.dma_start(offsets[:], offs)
         nc.sync.dma_start(weight[:, 0:256], wgt[:, 0:256])
         nc.sync.dma_start(xs[0][:], planes[0])
         nc.sync.dma_start(weight[:, 256:1024], wgt[:, 256:1024])
-        for q in range(4):
-            nc.gpsimd.dma_start(
-                r8s[32 * q : 32 * q + 4, :].bitcast(I32), r8_scales[0, 4 * q : 4 * q + 4, :].bitcast(I32)
-            )
-        for i in range(1, PACK):
-            nc.sync.dma_start(xs[i][:], planes[i])
-        for q in range(4):
-            nc.gpsimd.dma_start(
-                w4s[32 * q : 32 * q + 4, :].bitcast(I32), w4_scales[0, 4 * q : 4 * q + 4, :].bitcast(I32)
-            )
-        nc.sync.dma_start(r8[:].bitcast(I32), r8_words[0].rearrange("p n t -> p (n t)").bitcast(I32))
+        nc.sync.dma_start(xs[1][:], planes[1])
+        for q in range(3):
+            load_scales(nc.sync, r8s, r8_scales, q)
+        nc.sync.dma_start(xs[2][:], planes[2])
+        load_scales(nc.sync, r8s, r8_scales, 3)
+        for q in range(2):
+            load_scales(nc.sync, w4s, w4_scales, q)
+        nc.sync.dma_start(xs[3][:], planes[3])
+        for q in range(2, 4):
+            load_scales(nc.sync, w4s, w4_scales, q)
         nc.sync.dma_start(w4[:].bitcast(I32), w4_words[0].bitcast(I32))
+        nc.sync.dma_start(r8[:].bitcast(I32), r8_words[0].rearrange("p n t -> p (n t)").bitcast(I32))
 
         def gather(i, a, b):
             nc.vector.tensor_tensor(
@@ -81,15 +92,24 @@ def tile_list_heads_none_kernel(
                 interleave(nc.scalar.copy, 0, 0, 512)
                 interleave(nc.scalar.copy, 0, 512, 1024)
 
+        for a in range(512, 1024, 128):
+            for turn in range(2):
+                warm_up(g[1][:, 0, a : a + 128])
+
         chunks = ((0, 256, nc.scalar.copy), (256, 256, nc.scalar.copy), (512, 256, nc.scalar.copy), (768, 256, nc.vector.tensor_copy))
         for a, w, copy in chunks:
             gather(3, a, a + w)
+            if a < 512:
+                for b in range(a, a + 256, 128):
+                    for turn in range(2):
+                        warm_up(g[1][:, 1, b : b + 128])
             interleave(copy, 1, a, a + w)
-            nc.vector.quantize_mx(
-                out=codes[:, a : a + w].bitcast(FP8X4),
-                scales=scales[:, a : a + w],
-                in_=xb[:, a : a + w, :].rearrange("p n t -> p (n t)"),
-            )
+            for b in range(a, a + w, 128):
+                nc.vector.quantize_mx(
+                    out=codes[:, b : b + 128].bitcast(FP8X4),
+                    scales=scales[:, b : b + 128],
+                    in_=xb[:, b : b + 128, :].rearrange("p n t -> p (n t)"),
+                )
             for m in range(2):
                 acc = psum.tile([P, w], F32, name=f"acc{a}_{m}")
                 for b in range(0, w, 128):
@@ -113,7 +133,7 @@ def tile_list_heads_none_kernel(
                         stop=True,
                     )
                 res = keep.tile([P, w], F32, name=f"res{a}_{m}", align_bytes=64)
-                if m == 0:
+                if m == 0 or a < 512:
                     nc.scalar.copy(res[:], acc[:])
                 else:
                     nc.vector.tensor_copy(res[:], acc[:])

@@ -43,18 +43,14 @@ def tile_list_heads_none_kernel(
         codes = keep.tile([P, S], U32, name="codes", align_bytes=64)
         scales = keep.tile([P, S], U8, name="scales", align_bytes=64)
 
-        ident = keep.tile([P, P], F32, name="ident", align_bytes=64)
-        make_identity(nc, ident[:])
-        warm = psum.tile([P, 256], F32, name="acc768_1")
-
-        def warm_up(src):
-            nc.tensor.transpose(warm[:, 0:128], src, ident[:])
-
         nc.vector.memset(r8s[:].bitcast(I32), 0)
         nc.vector.memset(w4s[:].bitcast(I32), 0)
 
         def load_scales(engine, tile, src, q):
             engine.dma_start(tile[32 * q : 32 * q + 4, :].bitcast(I32), src[0, 4 * q : 4 * q + 4, :].bitcast(I32))
+
+        for q in range(4):
+            load_scales(nc.gpsimd, r8s, r8_scales, q)
 
         nc.sync.dma_start(offsets[:], offs)
         nc.sync.dma_start(weight[:, 0:256], wgt[:, 0:256])
@@ -62,16 +58,19 @@ def tile_list_heads_none_kernel(
         nc.sync.dma_start(weight[:, 256:1024], wgt[:, 256:1024])
         nc.sync.dma_start(xs[1][:], planes[1])
         for q in range(3):
-            load_scales(nc.sync, r8s, r8_scales, q)
+            load_scales(nc.sync, w4s, w4_scales, q)
         nc.sync.dma_start(xs[2][:], planes[2])
-        load_scales(nc.sync, r8s, r8_scales, 3)
-        for q in range(2):
-            load_scales(nc.sync, w4s, w4_scales, q)
+        load_scales(nc.sync, w4s, w4_scales, 3)
         nc.sync.dma_start(xs[3][:], planes[3])
-        for q in range(2, 4):
-            load_scales(nc.sync, w4s, w4_scales, q)
         nc.sync.dma_start(w4[:].bitcast(I32), w4_words[0].bitcast(I32))
         nc.sync.dma_start(r8[:].bitcast(I32), r8_words[0].rearrange("p n t -> p (n t)").bitcast(I32))
+
+        ident = keep.tile([P, P], F32, name="ident", align_bytes=64)
+        make_identity(nc, ident[:])
+        warm = psum.tile([P, 256], F32, name="acc768_1")
+
+        def warm_up(src):
+            nc.tensor.transpose(warm[:, 0:128], src, ident[:])
 
         def gather(i, a, b):
             nc.vector.tensor_tensor(
@@ -103,7 +102,8 @@ def tile_list_heads_none_kernel(
                 for b in range(a, a + 256, 128):
                     for turn in range(2):
                         warm_up(g[1][:, 1, b : b + 128])
-            interleave(copy, 1, a, a + w)
+            for b in range(a, a + w, 128 if a == 0 else w):
+                interleave(copy, 1, b, b + (128 if a == 0 else w))
             for b in range(a, a + w, 128):
                 nc.vector.quantize_mx(
                     out=codes[:, b : b + 128].bitcast(FP8X4),

from contextlib import ExitStack

import concourse.mybir as mybir
from concourse.masks import make_identity

K, M, T, S = 512, 256, 2048, 1024
FLOPS = 2 * 2 * K * M * S

F32 = mybir.dt.float32
BF16 = mybir.dt.bfloat16
I32 = mybir.dt.int32
U32 = mybir.dt.uint32
U16 = mybir.dt.uint16
U8 = mybir.dt.uint8
FP8X4 = mybir.dt.float8_e4m3fn_x4
FP4X4 = mybir.dt.float4_e2m1fn_x4
MULT = mybir.AluOpType.mult

P = 128
PACK = 4


def tile_list_heads_none_kernel(
    tc, xT, w4_words, w4_scales, r8_words, r8_scales, wgt, offs, out
):
    nc = tc.nc
    planes = xT.rearrange("(p i) t -> i p t", i=PACK)

    with ExitStack() as ctx:
        lists = ctx.enter_context(tc.tile_pool(name="lists", bufs=1))
        keep = ctx.enter_context(tc.tile_pool(name="keep", bufs=1))
        psum = ctx.enter_context(tc.psum_pool(name="psum", bufs=1))

        offsets = lists.tile([P, S // 16], U16, name="offsets")
        weight = keep.tile([P, S], F32, name="weight", align_bytes=64)
        xs = [keep.tile([P, T], F32, name=f"x{i}", align_bytes=64) for i in range(PACK)]
        w4 = keep.tile([P, 2 * M], U8, name="w4", align_bytes=64)
        r8 = keep.tile([P, M], U32, name="r8", align_bytes=64)
        w4s = keep.tile([P, M], U8, name="w4s", align_bytes=64)
        r8s = keep.tile([P, M], U8, name="r8s", align_bytes=64)
        g = [keep.tile([P, 2, S], F32, name=f"g{h}", align_bytes=64) for h in range(2)]
        xb = keep.tile([P, S, PACK], BF16, name="xb", align_bytes=64)
        codes = keep.tile([P, S], U32, name="codes", align_bytes=64)
        scales = keep.tile([P, S], U8, name="scales", align_bytes=64)

        nc.vector.memset(r8s[:].bitcast(I32), 0)
        nc.vector.memset(w4s[:].bitcast(I32), 0)

        def load_scales(engine, tile, src, q):
            engine.dma_start(tile[32 * q : 32 * q + 4, :].bitcast(I32), src[0, 4 * q : 4 * q + 4, :].bitcast(I32))

        for q in range(4):
            load_scales(nc.gpsimd, r8s, r8_scales, q)

        nc.sync.dma_start(offsets[:], offs)
        nc.sync.dma_start(weight[:, 0:256], wgt[:, 0:256])
        nc.sync.dma_start(xs[0][:], planes[0])
        nc.sync.dma_start(weight[:, 256:1024], wgt[:, 256:1024])
        nc.sync.dma_start(xs[1][:], planes[1])
        for q in range(3):
            load_scales(nc.sync, w4s, w4_scales, q)
        nc.sync.dma_start(xs[2][:], planes[2])
        load_scales(nc.sync, w4s, w4_scales, 3)
        nc.sync.dma_start(xs[3][:], planes[3])
        nc.sync.dma_start(w4[:].bitcast(I32), w4_words[0].bitcast(I32))
        nc.sync.dma_start(r8[:].bitcast(I32), r8_words[0].rearrange("p n t -> p (n t)").bitcast(I32))

        ident = keep.tile([P, P], F32, name="ident", align_bytes=64)
        make_identity(nc, ident[:])
        warm = psum.tile([P, 256], F32, name="acc768_1")

        def warm_up(src):
            nc.tensor.transpose(warm[:, 0:128], src, ident[:])

        def gather(i, a, b):
            nc.vector.tensor_tensor(
                g[i // 2][:, i % 2, a:b], xs[i][:].indirect(offsets[:, a // 16 : b // 16]), weight[:, a:b], MULT
            )

        def interleave(copy, h, a, b):
            copy(xb[:, a:b, 2 * h : 2 * h + 2], g[h][:, :, a:b].rearrange("p t n -> p n t"))

        for i in range(3):
            if i == 0:
                gather(i, 0, 256)
                gather(i, 256, 512)
            else:
                gather(i, 0, 512)
            gather(i, 512, 1024)
            if i == 1:
                interleave(nc.scalar.copy, 0, 0, 512)
                interleave(nc.scalar.copy, 0, 512, 1024)

        for a in range(512, 1024, 128):
            for turn in range(2):
                warm_up(g[1][:, 0, a : a + 128])

        chunks = ((0, 256, nc.scalar.copy), (256, 256, nc.scalar.copy), (512, 256, nc.scalar.copy), (768, 256, nc.vector.tensor_copy))
        for a, w, copy in chunks:
            gather(3, a, a + w)
            if a < 512:
                for b in range(a, a + 256, 128):
                    for turn in range(2):
                        warm_up(g[1][:, 1, b : b + 128])
            for b in range(a, a + w, 128 if a == 0 else w):
                interleave(copy, 1, b, b + (128 if a == 0 else w))
            for b in range(a, a + w, 128):
                nc.vector.quantize_mx(
                    out=codes[:, b : b + 128].bitcast(FP8X4),
                    scales=scales[:, b : b + 128],
                    in_=xb[:, b : b + 128, :].rearrange("p n t -> p (n t)"),
                )
            for m in range(2):
                acc = psum.tile([P, w], F32, name=f"acc{a}_{m}")
                for b in range(0, w, 128):
                    cols = slice(a + b, a + b + 128)
                    nc.tensor.matmul_mx(
                        out=acc[:, b : b + 128],
                        lhsT=w4[:, 256 * m : 256 * m + 256].bitcast(FP4X4),
                        lhsT_scale=w4s[:, 128 * m : 128 * m + 128],
                        rhs=codes[:, cols].bitcast(FP8X4),
                        rhs_scale=scales[:, cols],
                        start=True,
                        stop=False,
                    )
                    nc.tensor.matmul_mx(
                        out=acc[:, b : b + 128],
                        lhsT=r8[:, 128 * m : 128 * m + 128].bitcast(FP8X4),
                        lhsT_scale=r8s[:, 128 * m : 128 * m + 128],
                        rhs=codes[:, cols].bitcast(FP8X4),
                        rhs_scale=scales[:, cols],
                        start=False,
                        stop=True,
                    )
                res = keep.tile([P, w], F32, name=f"res{a}_{m}", align_bytes=64)
                if m == 0 or a < 512:
                    nc.scalar.copy(res[:], acc[:])
                else:
                    nc.vector.tensor_copy(res[:], acc[:])
                nc.sync.dma_start(out[128 * m : 128 * m + 128, a : a + w], res[:])
